import numpy as np
import ml_dtypes

BF16 = ml_dtypes.bfloat16


def bf(x):
    return np.asarray(x, np.float32).astype(BF16)


def f32(x):
    return np.asarray(x, np.float32)


def f64(x):
    return np.asarray(x).astype(np.float64)


def striped(idx):
    return np.concatenate([l.reshape(-1, 16).T for l in idx])


def rows(idx, k):
    return np.tile(np.repeat(idx, 16, axis=0), (k // (16 * 8), 1))


def look(tab, idx):
    return np.take_along_axis(f64(tab), rows(idx, len(tab)), axis=1)


K, S, V, N, M = 256, 2048, 1024, 1024, 256


def setup_inputs():
    return {"tab": f32(np.random.standard_normal((2, K, S))), "w": bf(np.random.standard_normal((K, M)) / np.sqrt(K)), "b": f32(0.5 * np.random.standard_normal((M, 1))), "offs": striped(np.stack([np.random.permutation(S)[:N] for _ in range(8)]))}


def reference(tab, w, b, offs):
    idx = np.stack([g.T.reshape(-1) for g in np.split(offs, 8)])
    x = 1.0 / (1.0 + np.exp(-look(tab[0], idx))) * np.tanh(look(tab[1], idx))
    y = f64(w).T @ x
    return np.maximum(y + f64(b), 0.0)

@@ -1,0 +1,71 @@
+import concourse.mybir as mybir
+
+F32, BF16, U16 = mybir.dt.float32, mybir.dt.bfloat16, mybir.dt.uint16
+SIGMOID, TANH = mybir.ActivationFunctionType.Sigmoid, mybir.ActivationFunctionType.Tanh
+ADD, MAX, MULT = mybir.AluOpType.add, mybir.AluOpType.max, mybir.AluOpType.mult
+
+P = 128
+ROWS, PLACES, PICKS, OUTS = 256, 2048, 1024, 256
+PIECE = 512
+ENTRIES_PER_COLUMN = 16
+
+FLOPS = 2 * ROWS * OUTS * PICKS
+
+
+def tile_lookup_cell_sigtanh_relu_kernel(tc, tab, w, b, offs, out):
+    nc = tc.nc
+    row_blocks, out_blocks, pieces = ROWS // P, OUTS // P, PICKS // PIECE
+    list_columns = PIECE // ENTRIES_PER_COLUMN
+
+    with (
+        tc.tile_pool(name="held", bufs=1) as held,
+        tc.tile_pool(name="picked", bufs=2) as picked,
+        tc.tile_pool(name="results", bufs=2) as results,
+        tc.psum_pool(name="sums", bufs=1) as sums,
+    ):
+        offsets = held.tile([P, PICKS // ENTRIES_PER_COLUMN], U16, name="offsets")
+        nc.sync.dma_start(offsets[:], offs)
+
+        gate, state = [], []
+        for k in range(row_blocks):
+            for name, table, windows in (("gate", 0, gate), ("state", 1, state)):
+                window = held.tile([P, PLACES], F32, name=f"{name}{k}")
+                nc.sync.dma_start(window[:], tab[table, k * P : (k + 1) * P, :])
+                windows.append(window)
+
+        weights = [held.tile([P, OUTS], BF16, name=f"weights{k}") for k in range(row_blocks)]
+        for k in range(row_blocks):
+            nc.sync.dma_start(weights[k][:], w[k * P : (k + 1) * P, :])
+        bias = [held.tile([P, 1], F32, name=f"bias{m}") for m in range(out_blocks)]
+        for m in range(out_blocks):
+            nc.sync.dma_start(bias[m][:], b[m * P : (m + 1) * P, :])
+
+        bank = [
+            [sums.tile([P, PIECE], F32, name=f"bank{m}_{s}") for s in range(pieces)] for m in range(out_blocks)
+        ]
+
+        for k in range(row_blocks):
+            sig, th = [], []
+            for func, window, values, name in ((SIGMOID, gate[k], sig, "sig"), (TANH, state[k], th, "th")):
+                for s in range(pieces):
+                    value = picked.tile([P, PIECE], F32, name=f"{name}{s}")
+                    picks = offsets[:, s * list_columns : (s + 1) * list_columns]
+                    nc.scalar.activation(value[:], window[:].indirect(picks), func)
+                    values.append(value)
+            for s in range(pieces):
+                x = picked.tile([P, PIECE], BF16, name=f"x{s}")
+                nc.vector.tensor_tensor(x[:], sig[s][:], th[s][:], MULT)
+                for m in range(out_blocks):
+                    nc.tensor.matmul(
+                        bank[m][s][:],
+                        weights[k][:, m * P : (m + 1) * P],
+                        x[:],
+                        start=(k == 0),
+                        stop=(k == row_blocks - 1),
+                    )
+
+        for s in range(pieces):
+            for m in range(out_blocks):
+                result = results.tile([P, PIECE], F32, name=f"result{m}")
+                nc.vector.tensor_scalar(result[:], bank[m][s][:], bias[m][:], 0.0, ADD, MAX)
+                nc.sync.dma_start(out[m * P : (m + 1) * P, s * PIECE : (s + 1) * PIECE], result[:])

@@ -23,6 +23,11 @@ def tile_lookup_cell_sigtanh_relu_kernel(tc, tab, w, b, offs, out):
         tc.tile_pool(name="results", bufs=2) as results,
         tc.psum_pool(name="sums", bufs=1) as sums,
     ):
+        zero = held.tile([P, 1], F32, name="zero")
+        nc.vector.memset(zero[:], 0.0)
+        warmed = held.tile([P, 1], F32, name="warmed")
+        nc.scalar.activation(warmed[:], zero[:], SIGMOID)
+
         offsets = held.tile([P, PICKS // ENTRIES_PER_COLUMN], U16, name="offsets")
         nc.sync.dma_start(offsets[:], offs)
 

@@ -1,13 +1,18 @@
+from contextlib import ExitStack
+
 import concourse.mybir as mybir
 
 F32, BF16, U16 = mybir.dt.float32, mybir.dt.bfloat16, mybir.dt.uint16
 SIGMOID, TANH = mybir.ActivationFunctionType.Sigmoid, mybir.ActivationFunctionType.Tanh
+RELU = mybir.ActivationFunctionType.Relu
 ADD, MAX, MULT = mybir.AluOpType.add, mybir.AluOpType.max, mybir.AluOpType.mult
 
 P = 128
 ROWS, PLACES, PICKS, OUTS = 256, 2048, 1024, 256
 PIECE = 512
+HALF = PIECE // 2
 ENTRIES_PER_COLUMN = 16
+BIAS_ROWS = 32
 
 FLOPS = 2 * ROWS * OUTS * PICKS
 
@@ -18,10 +23,10 @@ def tile_lookup_cell_sigtanh_relu_kernel(tc, tab, w, b, offs, out):
     list_columns = PIECE // ENTRIES_PER_COLUMN
 
     with (
+        ExitStack() as stack,
         tc.tile_pool(name="held", bufs=1) as held,
         tc.tile_pool(name="picked", bufs=2) as picked,
         tc.tile_pool(name="results", bufs=2) as results,
-        tc.psum_pool(name="sums", bufs=1) as sums,
     ):
         zero = held.tile([P, 1], F32, name="zero")
         nc.vector.memset(zero[:], 0.0)
@@ -31,22 +36,35 @@ def tile_lookup_cell_sigtanh_relu_kernel(tc, tab, w, b, offs, out):
         offsets = held.tile([P, PICKS // ENTRIES_PER_COLUMN], U16, name="offsets")
         nc.sync.dma_start(offsets[:], offs)
 
+        bias_row = held.tile([BIAS_ROWS, OUTS], F32, name="bias_row")
+        nc.vector.memset(bias_row[:], 0.0)
+
         gate, state = [], []
         for k in range(row_blocks):
             for name, table, windows in (("gate", 0, gate), ("state", 1, state)):
                 window = held.tile([P, PLACES], F32, name=f"{name}{k}")
                 nc.sync.dma_start(window[:], tab[table, k * P : (k + 1) * P, :])
                 windows.append(window)
+            if k == 0:
+                nc.sync.dma_start(bias_row[0:1, :], b.rearrange("m o -> o m"))
 
         weights = [held.tile([P, OUTS], BF16, name=f"weights{k}") for k in range(row_blocks)]
         for k in range(row_blocks):
             nc.sync.dma_start(weights[k][:], w[k * P : (k + 1) * P, :])
-        bias = [held.tile([P, 1], F32, name=f"bias{m}") for m in range(out_blocks)]
-        for m in range(out_blocks):
-            nc.sync.dma_start(bias[m][:], b[m * P : (m + 1) * P, :])
 
-        bank = [
-            [sums.tile([P, PIECE], F32, name=f"bank{m}_{s}") for s in range(pieces)] for m in range(out_blocks)
+        ones = held.tile([BIAS_ROWS, 1], F32, name="ones")
+        nc.vector.memset(ones[:], 1.0)
+        bias = held.tile([P, out_blocks], F32, name="bias")
+        with tc.psum_pool(name="turned", bufs=1) as turned:
+            column = turned.tile([P, out_blocks], F32, name="column")
+            for m in range(out_blocks):
+                nc.tensor.matmul(column[:, m : m + 1], bias_row[:, m * P : (m + 1) * P], ones[:], start=True, stop=True)
+            nc.vector.tensor_copy(bias[:], column[:])
+        sums = stack.enter_context(tc.psum_pool(name="sums", bufs=1))
+
+        sums_of = [
+            [[sums.tile([P, HALF], F32, name=f"sums{m}_{s}_{h}") for h in range(2)] for s in range(pieces)]
+            for m in range(out_blocks)
         ]
 
         for k in range(row_blocks):
@@ -58,19 +76,22 @@ def tile_lookup_cell_sigtanh_relu_kernel(tc, tab, w, b, offs, out):
                     nc.scalar.activation(value[:], window[:].indirect(picks), func)
                     values.append(value)
             for s in range(pieces):
-                x = picked.tile([P, PIECE], BF16, name=f"x{s}")
-                nc.vector.tensor_tensor(x[:], sig[s][:], th[s][:], MULT)
-                for m in range(out_blocks):
-                    nc.tensor.matmul(
-                        bank[m][s][:],
-                        weights[k][:, m * P : (m + 1) * P],
-                        x[:],
-                        start=(k == 0),
-                        stop=(k == row_blocks - 1),
-                    )
+                for h in range(2):
+                    half = slice(h * HALF, (h + 1) * HALF)
+                    x = picked.tile([P, HALF], BF16, name=f"x{s}_{h}")
+                    nc.vector.tensor_tensor(x[:], sig[s][:, half], th[s][:, half], MULT)
+                    for m in range(out_blocks):
+                        nc.tensor.matmul(
+                            sums_of[m][s][h][:],
+                            weights[k][:, m * P : (m + 1) * P],
+                            x[:],
+                            start=(k == 0),
+                            stop=(k == row_blocks - 1),
+                        )
 
         for s in range(pieces):
             for m in range(out_blocks):
                 result = results.tile([P, PIECE], F32, name=f"result{m}")
-                nc.vector.tensor_scalar(result[:], bank[m][s][:], bias[m][:], 0.0, ADD, MAX)
+                nc.scalar.activation(result[:, :HALF], sums_of[m][s][0][:], RELU, bias=bias[:, m : m + 1])
+                nc.vector.tensor_scalar(result[:, HALF:], sums_of[m][s][1][:], bias[:, m : m + 1], 0.0, ADD, MAX)
                 nc.sync.dma_start(out[m * P : (m + 1) * P, s * PIECE : (s + 1) * PIECE], result[:])

from contextlib import ExitStack

import concourse.mybir as mybir

F32, BF16, U16 = mybir.dt.float32, mybir.dt.bfloat16, mybir.dt.uint16
SIGMOID, TANH = mybir.ActivationFunctionType.Sigmoid, mybir.ActivationFunctionType.Tanh
RELU = mybir.ActivationFunctionType.Relu
ADD, MAX, MULT = mybir.AluOpType.add, mybir.AluOpType.max, mybir.AluOpType.mult

P = 128
ROWS, PLACES, PICKS, OUTS = 256, 2048, 1024, 256
PIECE = 512
HALF = PIECE // 2
ENTRIES_PER_COLUMN = 16
BIAS_ROWS = 32

FLOPS = 2 * ROWS * OUTS * PICKS


def tile_lookup_cell_sigtanh_relu_kernel(tc, tab, w, b, offs, out):
    nc = tc.nc
    row_blocks, out_blocks, pieces = ROWS // P, OUTS // P, PICKS // PIECE
    list_columns = PIECE // ENTRIES_PER_COLUMN

    with (
        ExitStack() as stack,
        tc.tile_pool(name="held", bufs=1) as held,
        tc.tile_pool(name="picked", bufs=2) as picked,
        tc.tile_pool(name="results", bufs=2) as results,
    ):
        zero = held.tile([P, 1], F32, name="zero")
        nc.vector.memset(zero[:], 0.0)
        warmed = held.tile([P, 1], F32, name="warmed")
        nc.scalar.activation(warmed[:], zero[:], SIGMOID)

        offsets = held.tile([P, PICKS // ENTRIES_PER_COLUMN], U16, name="offsets")
        nc.sync.dma_start(offsets[:], offs)

        bias_row = held.tile([BIAS_ROWS, OUTS], F32, name="bias_row")
        nc.vector.memset(bias_row[:], 0.0)

        gate, state = [], []
        for k in range(row_blocks):
            for name, table, windows in (("gate", 0, gate), ("state", 1, state)):
                window = held.tile([P, PLACES], F32, name=f"{name}{k}")
                nc.sync.dma_start(window[:], tab[table, k * P : (k + 1) * P, :])
                windows.append(window)
            if k == 0:
                nc.sync.dma_start(bias_row[0:1, :], b.rearrange("m o -> o m"))

        weights = [held.tile([P, OUTS], BF16, name=f"weights{k}") for k in range(row_blocks)]
        for k in range(row_blocks):
            nc.sync.dma_start(weights[k][:], w[k * P : (k + 1) * P, :])

        ones = held.tile([BIAS_ROWS, 1], F32, name="ones")
        nc.vector.memset(ones[:], 1.0)
        bias = held.tile([P, out_blocks], F32, name="bias")
        with tc.psum_pool(name="turned", bufs=1) as turned:
            column = turned.tile([P, out_blocks], F32, name="column")
            for m in range(out_blocks):
                nc.tensor.matmul(column[:, m : m + 1], bias_row[:, m * P : (m + 1) * P], ones[:], start=True, stop=True)
            nc.vector.tensor_copy(bias[:], column[:])
        sums = stack.enter_context(tc.psum_pool(name="sums", bufs=1))

        sums_of = [
            [[sums.tile([P, HALF], F32, name=f"sums{m}_{s}_{h}") for h in range(2)] for s in range(pieces)]
            for m in range(out_blocks)
        ]

        for k in range(row_blocks):
            sig, th = [], []
            for func, window, values, name in ((SIGMOID, gate[k], sig, "sig"), (TANH, state[k], th, "th")):
                for s in range(pieces):
                    value = picked.tile([P, PIECE], F32, name=f"{name}{s}")
                    picks = offsets[:, s * list_columns : (s + 1) * list_columns]
                    nc.scalar.activation(value[:], window[:].indirect(picks), func)
                    values.append(value)
            for s in range(pieces):
                for h in range(2):
                    half = slice(h * HALF, (h + 1) * HALF)
                    x = picked.tile([P, HALF], BF16, name=f"x{s}_{h}")
                    nc.vector.tensor_tensor(x[:], sig[s][:, half], th[s][:, half], MULT)
                    for m in range(out_blocks):
                        nc.tensor.matmul(
                            sums_of[m][s][h][:],
                            weights[k][:, m * P : (m + 1) * P],
                            x[:],
                            start=(k == 0),
                            stop=(k == row_blocks - 1),
                        )

        for s in range(pieces):
            for m in range(out_blocks):
                result = results.tile([P, PIECE], F32, name=f"result{m}")
                nc.scalar.activation(result[:, :HALF], sums_of[m][s][0][:], RELU, bias=bias[:, m : m + 1])
                nc.vector.tensor_scalar(result[:, HALF:], sums_of[m][s][1][:], bias[:, m : m + 1], 0.0, ADD, MAX)
                nc.sync.dma_start(out[m * P : (m + 1) * P, s * PIECE : (s + 1) * PIECE], result[:])
